import numpy as np
CORES = [72,73,74,75,76,77,78,79,64,65,66,67]
N = 12
T = 512
ROUTE = [[[8],[1],[5],[1],[7],[4],[1],[4],[9],[8],[10],[4],[0],[0],[3],[10],[0],[5],[1],[3],[10],[6],[6],[6],[8],[0],[7],[6],[3],[6],[9],[8],[4],[6],[4],[9],[1],[10],[10],[3],[5],[9],[5],[10],[5],[9],[10],[5],[10],[7],[10],[0],[11],[0],[2],[0],[6],[11],[2],[10],[4],[10],[1],[1],[11],[3],[1],[9],[11],[8],[8],[7],[1],[7],[11],[9],[1],[8],[3],[2],[6],[0],[1],[9],[0],[7],[10],[1],[1],[7],[0],[3],[11],[1],[4],[2],[8],[9],[2],[10],[7],[7],[8],[7],[11],[9],[11],[0],[4],[3],[4],[7],[11],[0],[7],[0],[6],[11],[4],[0],[1],[10],[7],[2],[1],[6],[4],[6],[0],[6],[3],[2],[7],[3],[7],[6],[4],[9],[5],[5],[6],[1],[11],[2],[0],[3],[2],[10],[10],[10],[4],[8],[10],[6],[4],[7],[4],[7],[2],[6],[5],[6],[2],[7],[4],[5],[3],[1],[10],[6],[9],[3],[0],[4],[2],[11],[4],[10],[6],[0],[6],[4],[0],[5],[4],[3],[1],[9],[7],[5],[9],[4],[8],[7],[4],[6],[6],[8],[11],[4],[0],[4],[6],[8],[7],[10],[7],[11],[11],[8],[8],[7],[5],[0],[11],[5],[7],[3],[5],[5],[11],[3],[9],[4],[1],[2],[6],[7],[11],[5],[1],[3],[5],[2],[10],[4],[11],[3],[11],[0],[4],[1],[10],[5],[0],[0],[8],[4],[9],[0],[8],[2],[4],[8],[5],[4],[7],[11],[11],[7],[2],[4],[5],[10],[8],[11],[10],[10],[4],[5],[0],[3],[4],[6],[0],[7],[1],[11],[11],[9],[10],[5],[9],[4],[11],[10],[1],[4],[7],[2],[3],[2],[1],[2],[1],[11],[10],[8],[8],[10],[4],[9],[9],[6],[2],[3],[1],[1],[0],[9],[11],[7],[11],[3],[9],[3],[9],[8],[8],[7],[7],[5],[8],[3],[8],[0],[9],[10],[2],[8],[5],[4],[6],[9],[8],[3],[10],[5],[8],[11],[1],[9],[11],[1],[9],[1],[0],[10],[5],[11],[8],[10],[1],[4],[4],[11],[1],[0],[0],[4],[11],[8],[0],[5],[5],[2],[4],[7],[1],[5],[5],[0],[1],[3],[1],[0],[0],[7],[3],[7],[4],[9],[8],[1],[10],[11],[0],[8],[0],[1],[0],[7],[10],[2],[5],[5],[3],[10],[3],[7],[2],[2],[10],[4],[5],[5],[7],[7],[1],[1],[5],[3],[6],[6],[1],[0],[7],[0],[4],[4],[7],[1],[0],[8],[5],[4],[0],[11],[1],[1],[2],[5],[8],[2],[5],[1],[8],[7],[2],[10],[6],[11],[10],[1],[7],[9],[5],[1],[11],[0],[0],[8],[1],[1],[7],[9],[4],[11],[2],[2],[10],[2],[0],[5],[7],[9],[2],[1],[1],[6],[3],[7],[5],[9],[11],[11],[9],[6],[1],[3],[7],[6],[8],[8],[5],[10],[2],[11],[2],[9],[11],[0],[3],[3],[9],[9],[1],[8],[4],[4],[2],[3],[5],[1],[5],[7],[2],[0],[6],[0],[4],[2]],[[1],[4],[7],[3],[0],[9],[6],[10],[6],[1],[0],[4],[3],[7],[3],[3],[11],[4],[2],[4],[7],[3],[5],[0],[0],[10],[10],[9],[6],[7],[2],[4],[2],[6],[4],[2],[5],[2],[2],[10],[11],[0],[0],[1],[10],[6],[4],[1],[0],[2],[7],[5],[1],[0],[9],[6],[11],[3],[5],[7],[11],[4],[11],[8],[3],[10],[10],[9],[6],[1],[5],[4],[3],[8],[9],[7],[8],[10],[3],[3],[8],[2],[5],[10],[11],[9],[6],[11],[5],[4],[2],[1],[3],[11],[4],[10],[3],[9],[11],[7],[1],[1],[8],[5],[9],[4],[9],[3],[7],[9],[1],[5],[2],[11],[4],[0],[11],[4],[8],[7],[2],[4],[6],[2],[1],[8],[10],[0],[11],[5],[2],[2],[8],[4],[2],[2],[7],[4],[3],[4],[3],[8],[0],[2],[1],[9],[3],[4],[3],[9],[1],[2],[4],[10],[1],[2],[0],[9],[10],[0],[4],[5],[3],[2],[7],[11],[9],[8],[3],[6],[11],[10],[10],[2],[10],[4],[1],[0],[2],[5],[0],[1],[10],[11],[2],[9],[7],[4],[4],[1],[7],[5],[4],[7],[2],[6],[11],[8],[10],[0],[7],[4],[2],[11],[0],[9],[2],[4],[8],[1],[9],[9],[1],[1],[0],[5],[0],[2],[2],[1],[1],[3],[0],[4],[6],[6],[7],[4],[9],[2],[8],[6],[8],[11],[7],[8],[10],[0],[1],[7],[11],[10],[10],[1],[6],[11],[0],[1],[11],[11],[1],[2],[10],[3],[0],[3],[11],[4],[4],[8],[3],[0],[3],[9],[3],[4],[6],[5],[3],[1],[9],[4],[3],[11],[7],[9],[2],[8],[6],[9],[11],[0],[10],[10],[8],[3],[4],[0],[11],[9],[6],[11],[0],[10],[3],[10],[8],[11],[7],[1],[10],[3],[2],[0],[7],[9],[9],[9],[5],[5],[1],[8],[11],[11],[10],[0],[3],[2],[7],[2],[2],[3],[8],[5],[7],[0],[3],[3],[1],[8],[0],[7],[10],[3],[7],[1],[2],[2],[10],[4],[2],[8],[5],[2],[5],[3],[4],[4],[5],[7],[10],[5],[8],[11],[2],[7],[7],[10],[4],[8],[7],[8],[5],[9],[5],[2],[2],[0],[5],[8],[4],[5],[10],[5],[4],[9],[8],[1],[7],[11],[10],[8],[7],[6],[7],[9],[2],[0],[8],[4],[3],[7],[6],[3],[3],[2],[4],[10],[3],[7],[9],[8],[8],[11],[5],[8],[10],[8],[9],[5],[10],[0],[2],[6],[0],[3],[7],[10],[7],[7],[5],[1],[5],[1],[10],[7],[4],[4],[6],[6],[4],[2],[8],[2],[3],[5],[6],[11],[3],[3],[5],[11],[11],[10],[10],[5],[0],[2],[1],[9],[0],[6],[0],[1],[4],[1],[0],[5],[5],[3],[4],[1],[10],[5],[8],[3],[6],[5],[3],[10],[1],[1],[9],[8],[11],[7],[8],[9],[3],[1],[6],[9],[8],[3],[2],[1],[10],[1],[8],[2],[6],[10],[10],[1],[9],[11],[11],[4],[3],[7],[8],[9],[0],[3],[9],[3],[7],[4],[2],[8],[9],[2]],[[7],[5],[6],[9],[8],[6],[1],[7],[3],[6],[3],[9],[6],[3],[7],[10],[4],[2],[0],[2],[11],[0],[8],[7],[10],[7],[0],[4],[9],[8],[11],[2],[7],[1],[10],[10],[9],[10],[1],[9],[10],[7],[4],[9],[5],[1],[3],[10],[3],[2],[0],[5],[5],[11],[1],[3],[5],[8],[3],[7],[1],[1],[0],[11],[11],[8],[7],[3],[7],[1],[6],[11],[7],[8],[9],[0],[9],[0],[3],[6],[3],[10],[0],[4],[8],[11],[5],[7],[6],[1],[6],[10],[10],[10],[7],[6],[7],[1],[6],[3],[1],[8],[4],[3],[8],[0],[10],[11],[3],[3],[8],[4],[9],[8],[4],[7],[10],[11],[11],[11],[0],[5],[1],[1],[6],[4],[8],[8],[9],[2],[4],[6],[3],[4],[0],[1],[6],[1],[10],[7],[10],[8],[11],[6],[6],[0],[0],[0],[9],[10],[9],[1],[11],[7],[7],[11],[6],[6],[7],[7],[2],[5],[2],[0],[9],[5],[4],[7],[3],[2],[11],[4],[3],[0],[2],[4],[0],[1],[6],[10],[11],[8],[3],[1],[8],[11],[0],[3],[5],[7],[6],[8],[6],[11],[4],[0],[2],[11],[8],[11],[7],[10],[8],[0],[7],[4],[11],[3],[4],[2],[9],[0],[9],[2],[9],[11],[0],[11],[9],[9],[11],[1],[8],[10],[7],[11],[3],[6],[1],[0],[0],[5],[6],[0],[1],[0],[0],[5],[4],[1],[5],[1],[8],[2],[5],[6],[1],[0],[7],[2],[4],[10],[8],[1],[11],[3],[10],[8],[11],[0],[5],[11],[10],[1],[0],[3],[2],[8],[7],[1],[10],[6],[8],[4],[8],[0],[11],[1],[3],[1],[8],[2],[11],[0],[1],[5],[2],[1],[7],[10],[2],[3],[5],[2],[3],[8],[6],[2],[2],[8],[11],[8],[9],[4],[11],[1],[5],[8],[3],[5],[11],[5],[8],[9],[1],[3],[7],[3],[1],[8],[10],[6],[11],[4],[2],[3],[4],[7],[3],[8],[2],[0],[2],[6],[11],[6],[11],[4],[9],[2],[7],[8],[2],[3],[5],[9],[2],[5],[5],[6],[3],[7],[9],[0],[7],[5],[10],[11],[3],[5],[6],[1],[2],[8],[5],[3],[7],[1],[1],[2],[6],[4],[8],[8],[1],[7],[8],[3],[4],[7],[9],[7],[10],[9],[4],[8],[10],[4],[6],[4],[10],[5],[4],[8],[10],[9],[10],[9],[11],[6],[6],[6],[5],[4],[10],[3],[3],[0],[3],[4],[3],[8],[8],[6],[8],[0],[2],[5],[0],[8],[1],[8],[7],[4],[11],[7],[9],[6],[10],[6],[5],[7],[0],[0],[11],[3],[7],[8],[6],[5],[0],[6],[4],[3],[2],[10],[7],[3],[9],[8],[10],[9],[11],[6],[11],[8],[4],[2],[6],[5],[4],[11],[10],[11],[2],[2],[10],[3],[5],[7],[0],[0],[5],[9],[8],[8],[7],[9],[0],[3],[8],[11],[4],[7],[4],[3],[4],[7],[1],[8],[3],[2],[6],[1],[6],[3],[3],[2],[8],[7],[7],[1],[10],[1],[10],[7],[9],[4],[4],[1],[11],[10]],[[7],[2],[1],[2],[3],[11],[6],[6],[3],[9],[9],[7],[6],[9],[2],[0],[7],[8],[8],[0],[0],[11],[5],[10],[4],[1],[10],[8],[7],[6],[11],[11],[0],[10],[9],[5],[5],[6],[9],[9],[11],[6],[7],[1],[9],[11],[4],[0],[0],[9],[7],[0],[4],[3],[9],[6],[7],[6],[9],[8],[10],[10],[1],[3],[0],[8],[0],[5],[4],[2],[5],[9],[5],[10],[11],[2],[10],[11],[9],[2],[3],[3],[6],[2],[3],[3],[3],[6],[10],[0],[7],[6],[2],[6],[11],[0],[11],[1],[9],[10],[0],[0],[8],[6],[10],[10],[3],[2],[8],[8],[8],[10],[6],[1],[3],[6],[4],[7],[8],[4],[7],[11],[4],[3],[6],[3],[0],[0],[0],[4],[3],[5],[1],[7],[11],[8],[2],[7],[6],[0],[0],[11],[5],[5],[11],[2],[0],[4],[10],[9],[9],[7],[5],[10],[5],[8],[5],[5],[11],[10],[7],[8],[3],[2],[10],[11],[10],[4],[6],[0],[0],[10],[10],[7],[5],[8],[11],[4],[11],[6],[9],[11],[6],[7],[2],[10],[7],[0],[9],[11],[0],[5],[3],[6],[2],[5],[2],[10],[2],[1],[11],[3],[3],[3],[6],[8],[1],[5],[4],[11],[6],[0],[11],[11],[9],[1],[11],[11],[7],[8],[10],[7],[5],[6],[1],[11],[11],[5],[7],[7],[5],[10],[0],[4],[2],[6],[8],[5],[9],[7],[9],[10],[10],[5],[0],[4],[0],[7],[0],[8],[5],[5],[2],[5],[3],[5],[3],[11],[4],[0],[1],[8],[2],[1],[1],[2],[2],[3],[8],[7],[8],[11],[6],[0],[7],[9],[4],[2],[3],[8],[6],[10],[10],[1],[7],[4],[1],[2],[5],[10],[0],[11],[2],[3],[5],[10],[2],[0],[6],[7],[6],[0],[0],[4],[1],[6],[4],[6],[4],[5],[11],[2],[7],[1],[5],[10],[3],[3],[0],[3],[0],[1],[3],[7],[9],[11],[10],[11],[4],[1],[8],[9],[2],[5],[4],[7],[5],[9],[10],[3],[2],[4],[10],[10],[10],[3],[11],[7],[8],[1],[1],[6],[6],[0],[8],[4],[1],[11],[8],[7],[2],[10],[6],[0],[0],[7],[2],[5],[5],[2],[10],[8],[3],[0],[5],[4],[11],[7],[3],[8],[0],[9],[1],[7],[9],[11],[6],[1],[11],[7],[10],[1],[3],[9],[8],[7],[11],[5],[0],[6],[10],[6],[7],[3],[6],[2],[0],[9],[9],[9],[7],[7],[0],[1],[9],[11],[3],[4],[4],[5],[9],[4],[0],[2],[9],[10],[7],[0],[4],[3],[9],[2],[4],[7],[1],[1],[2],[9],[7],[3],[4],[4],[7],[8],[2],[5],[11],[8],[1],[8],[11],[3],[6],[4],[4],[6],[6],[6],[8],[8],[5],[9],[1],[10],[5],[1],[2],[5],[6],[3],[11],[0],[0],[1],[6],[8],[4],[4],[5],[2],[1],[5],[7],[9],[2],[3],[11],[9],[4],[7],[5],[0],[10],[2],[11],[0],[5],[3],[10],[7],[1],[10],[10],[0],[9],[1],[10],[2],[1],[4],[5],[2]],[[0],[4],[9],[3],[4],[5],[11],[10],[6],[4],[0],[9],[9],[0],[10],[9],[10],[9],[8],[4],[11],[7],[8],[6],[7],[7],[7],[9],[8],[1],[9],[11],[6],[9],[0],[3],[8],[9],[4],[9],[7],[11],[10],[7],[4],[8],[2],[1],[9],[3],[2],[6],[6],[3],[5],[2],[7],[4],[9],[3],[8],[3],[5],[7],[7],[1],[1],[0],[3],[10],[7],[1],[1],[2],[5],[8],[0],[11],[2],[9],[2],[1],[10],[11],[1],[8],[7],[7],[7],[3],[9],[9],[4],[2],[8],[9],[5],[8],[6],[10],[0],[6],[6],[5],[7],[9],[11],[2],[1],[5],[5],[3],[7],[3],[2],[6],[3],[9],[5],[0],[2],[11],[11],[5],[0],[1],[9],[1],[3],[11],[5],[7],[11],[1],[6],[6],[10],[0],[9],[5],[0],[8],[3],[3],[4],[8],[9],[3],[7],[9],[6],[2],[10],[4],[6],[10],[8],[7],[11],[9],[6],[10],[3],[2],[9],[6],[9],[11],[4],[8],[10],[11],[6],[1],[1],[1],[1],[8],[11],[7],[3],[7],[7],[0],[0],[11],[10],[6],[0],[7],[3],[5],[1],[7],[4],[6],[2],[1],[4],[3],[5],[8],[8],[10],[9],[4],[6],[1],[6],[0],[7],[6],[10],[0],[2],[8],[0],[8],[8],[4],[0],[8],[1],[0],[7],[5],[11],[9],[10],[7],[6],[4],[2],[4],[5],[6],[9],[10],[0],[1],[9],[11],[7],[8],[2],[3],[6],[8],[11],[7],[4],[4],[10],[10],[1],[11],[5],[5],[2],[1],[9],[5],[6],[4],[4],[1],[2],[9],[9],[2],[4],[0],[11],[4],[1],[9],[1],[10],[4],[9],[3],[11],[3],[2],[1],[11],[8],[9],[6],[4],[10],[11],[2],[0],[8],[11],[8],[5],[7],[11],[2],[9],[3],[9],[7],[2],[9],[2],[4],[5],[7],[11],[1],[8],[5],[7],[11],[6],[7],[3],[11],[2],[2],[2],[6],[5],[1],[9],[5],[6],[4],[0],[5],[7],[5],[1],[6],[2],[1],[9],[7],[1],[11],[10],[3],[11],[7],[3],[9],[11],[0],[5],[1],[3],[4],[9],[11],[5],[1],[4],[9],[1],[4],[5],[3],[3],[8],[2],[7],[3],[3],[8],[10],[8],[4],[1],[3],[9],[2],[6],[3],[8],[8],[9],[2],[7],[4],[5],[2],[3],[4],[4],[3],[10],[10],[2],[0],[2],[7],[4],[9],[4],[11],[0],[1],[0],[11],[4],[2],[7],[3],[7],[5],[5],[9],[4],[4],[2],[5],[6],[5],[8],[1],[4],[2],[10],[8],[4],[9],[7],[6],[3],[0],[6],[11],[5],[7],[0],[3],[6],[7],[7],[6],[2],[11],[2],[0],[9],[5],[10],[6],[1],[3],[10],[4],[3],[4],[5],[3],[4],[1],[7],[1],[7],[6],[2],[11],[5],[0],[4],[10],[7],[3],[7],[6],[1],[1],[2],[7],[8],[4],[2],[7],[1],[3],[10],[7],[6],[5],[10],[0],[7],[0],[10],[2],[6],[9],[1],[9],[10],[5],[1],[3],[11],[9],[1],[5],[6],[6],[7],[9],[5]],[[2],[11],[0],[8],[4],[3],[1],[10],[6],[6],[11],[10],[3],[3],[6],[11],[0],[8],[2],[7],[7],[0],[3],[11],[8],[3],[1],[8],[5],[5],[7],[9],[2],[11],[8],[10],[8],[1],[5],[4],[2],[2],[3],[3],[4],[1],[4],[1],[6],[11],[11],[9],[3],[5],[7],[4],[2],[9],[2],[10],[1],[4],[4],[8],[5],[11],[7],[4],[2],[10],[7],[1],[2],[2],[11],[10],[3],[5],[4],[3],[10],[6],[6],[2],[0],[0],[5],[2],[0],[11],[2],[10],[4],[5],[1],[6],[0],[4],[8],[6],[8],[11],[10],[1],[5],[9],[9],[11],[7],[5],[1],[2],[7],[11],[9],[3],[0],[9],[3],[1],[1],[8],[10],[3],[8],[1],[11],[0],[9],[11],[8],[9],[9],[7],[7],[8],[5],[1],[3],[5],[1],[11],[0],[5],[7],[2],[3],[9],[2],[9],[10],[4],[0],[8],[8],[8],[7],[2],[7],[9],[4],[0],[4],[3],[5],[7],[4],[0],[5],[8],[4],[6],[4],[2],[5],[7],[5],[11],[5],[5],[6],[5],[2],[3],[10],[1],[11],[11],[11],[10],[6],[7],[2],[10],[11],[7],[11],[0],[1],[6],[1],[2],[6],[8],[5],[7],[5],[1],[2],[0],[10],[1],[2],[0],[0],[3],[7],[2],[8],[8],[6],[0],[6],[2],[3],[0],[11],[0],[4],[5],[10],[10],[9],[9],[11],[11],[11],[10],[1],[3],[3],[3],[6],[5],[8],[8],[2],[3],[0],[1],[9],[9],[2],[3],[0],[0],[1],[3],[3],[5],[11],[10],[6],[1],[9],[0],[7],[9],[3],[5],[11],[2],[10],[9],[5],[7],[9],[2],[7],[10],[4],[10],[9],[6],[0],[4],[7],[4],[9],[1],[7],[7],[7],[3],[9],[6],[5],[9],[7],[6],[2],[4],[7],[5],[4],[2],[5],[2],[7],[10],[4],[9],[7],[6],[4],[8],[9],[10],[7],[4],[9],[10],[3],[10],[3],[6],[10],[10],[7],[8],[0],[1],[3],[11],[0],[6],[11],[2],[9],[7],[3],[8],[10],[0],[5],[10],[4],[7],[0],[7],[3],[10],[4],[9],[3],[10],[0],[1],[4],[2],[6],[0],[9],[6],[8],[0],[7],[8],[11],[10],[5],[4],[10],[8],[0],[9],[6],[10],[2],[8],[0],[0],[2],[6],[4],[7],[1],[11],[4],[9],[4],[8],[3],[11],[5],[0],[1],[0],[10],[9],[1],[2],[4],[5],[6],[8],[3],[9],[9],[0],[8],[8],[4],[0],[3],[1],[8],[5],[6],[9],[2],[8],[4],[3],[10],[8],[11],[1],[2],[9],[9],[8],[11],[9],[1],[1],[2],[7],[0],[5],[5],[1],[6],[9],[8],[10],[4],[7],[8],[9],[8],[3],[10],[10],[4],[7],[7],[3],[1],[7],[2],[2],[9],[2],[0],[3],[4],[3],[5],[8],[11],[11],[2],[3],[8],[10],[11],[1],[6],[10],[4],[0],[4],[10],[8],[6],[10],[10],[0],[2],[3],[7],[6],[3],[10],[7],[6],[5],[5],[5],[8],[4],[1],[3],[10],[2],[9],[3],[2],[11],[0],[2]],[[7],[4],[8],[6],[0],[3],[3],[8],[2],[2],[4],[6],[10],[1],[8],[5],[5],[6],[2],[2],[8],[3],[11],[9],[4],[6],[1],[8],[9],[2],[9],[10],[1],[6],[0],[9],[7],[5],[0],[1],[0],[6],[5],[8],[6],[9],[1],[7],[9],[7],[0],[6],[0],[9],[3],[9],[9],[9],[2],[11],[6],[8],[0],[5],[5],[11],[3],[1],[9],[9],[5],[3],[10],[0],[8],[10],[6],[9],[11],[10],[3],[11],[8],[1],[0],[6],[8],[7],[2],[9],[5],[1],[10],[5],[5],[8],[11],[10],[9],[3],[6],[9],[5],[9],[11],[10],[1],[4],[6],[5],[4],[1],[7],[6],[5],[2],[10],[3],[11],[11],[7],[3],[8],[5],[6],[2],[11],[10],[2],[1],[8],[9],[1],[4],[3],[2],[6],[7],[10],[11],[0],[4],[0],[10],[9],[3],[10],[1],[11],[1],[2],[0],[1],[11],[6],[2],[5],[9],[2],[0],[9],[8],[3],[3],[0],[10],[10],[4],[0],[10],[0],[2],[7],[4],[6],[8],[7],[11],[4],[8],[3],[4],[1],[8],[8],[5],[5],[3],[2],[7],[8],[9],[3],[6],[9],[5],[9],[10],[11],[9],[9],[8],[0],[11],[10],[2],[10],[7],[9],[5],[11],[6],[8],[5],[5],[5],[2],[11],[2],[1],[11],[5],[3],[5],[8],[2],[10],[8],[0],[0],[8],[2],[9],[10],[2],[2],[0],[7],[8],[5],[2],[5],[10],[1],[2],[6],[1],[5],[8],[10],[11],[6],[7],[1],[10],[9],[6],[11],[9],[10],[6],[10],[1],[5],[3],[8],[9],[8],[11],[7],[5],[11],[6],[10],[10],[3],[5],[10],[1],[10],[9],[6],[2],[2],[4],[3],[10],[1],[8],[0],[7],[2],[11],[2],[5],[0],[0],[9],[7],[2],[7],[2],[5],[3],[11],[7],[9],[2],[2],[9],[5],[10],[6],[9],[2],[7],[6],[1],[11],[6],[6],[4],[5],[3],[7],[0],[0],[9],[0],[7],[9],[1],[9],[4],[0],[4],[3],[0],[11],[7],[8],[8],[7],[9],[11],[9],[3],[11],[2],[3],[9],[7],[10],[8],[7],[2],[4],[6],[3],[4],[6],[0],[6],[3],[11],[2],[4],[8],[4],[11],[8],[2],[0],[4],[9],[1],[6],[0],[6],[9],[3],[2],[7],[2],[4],[10],[7],[0],[5],[8],[4],[4],[9],[7],[7],[1],[7],[1],[5],[9],[4],[2],[10],[7],[10],[11],[11],[10],[11],[0],[6],[10],[9],[2],[5],[9],[0],[7],[7],[2],[5],[11],[8],[9],[1],[9],[5],[0],[4],[8],[5],[7],[4],[3],[0],[6],[3],[9],[0],[7],[0],[4],[2],[9],[4],[5],[2],[7],[10],[10],[2],[2],[0],[8],[4],[8],[4],[8],[1],[8],[3],[3],[11],[2],[5],[6],[11],[3],[6],[10],[5],[5],[10],[6],[2],[9],[1],[4],[7],[0],[2],[7],[6],[11],[8],[10],[9],[11],[4],[5],[6],[7],[1],[5],[3],[3],[5],[3],[9],[7],[2],[10],[8],[1],[7],[0],[1],[10],[0],[11],[0],[3]],[[3],[1],[2],[9],[4],[10],[8],[2],[9],[4],[8],[9],[3],[6],[3],[1],[9],[0],[5],[11],[4],[8],[0],[10],[9],[1],[5],[3],[10],[2],[2],[10],[7],[1],[10],[10],[8],[7],[11],[7],[4],[7],[9],[8],[9],[0],[9],[1],[8],[0],[1],[4],[10],[3],[6],[1],[11],[11],[7],[11],[7],[9],[9],[5],[6],[9],[1],[4],[2],[8],[4],[10],[10],[2],[8],[10],[4],[2],[6],[6],[6],[1],[0],[2],[3],[0],[9],[0],[5],[0],[7],[0],[6],[9],[3],[3],[11],[9],[11],[2],[10],[7],[5],[8],[7],[2],[4],[1],[9],[1],[9],[5],[1],[11],[7],[6],[6],[3],[2],[0],[6],[5],[11],[5],[8],[4],[5],[9],[8],[10],[4],[6],[3],[1],[2],[8],[5],[4],[8],[7],[2],[5],[5],[7],[10],[10],[9],[6],[1],[3],[9],[2],[5],[3],[11],[9],[2],[11],[1],[11],[8],[8],[1],[3],[2],[1],[0],[7],[9],[4],[3],[4],[1],[7],[5],[10],[4],[7],[9],[1],[5],[1],[5],[11],[8],[9],[9],[5],[9],[9],[11],[0],[4],[7],[4],[8],[7],[11],[5],[11],[7],[7],[6],[5],[6],[11],[4],[8],[6],[3],[5],[1],[7],[4],[8],[6],[6],[5],[1],[8],[7],[9],[11],[10],[2],[8],[5],[3],[5],[7],[5],[0],[5],[0],[1],[5],[2],[6],[5],[3],[9],[7],[5],[5],[10],[11],[2],[1],[11],[1],[8],[6],[3],[10],[10],[8],[0],[3],[4],[9],[2],[11],[9],[11],[2],[6],[9],[11],[3],[11],[4],[8],[3],[10],[0],[6],[3],[10],[8],[8],[7],[7],[4],[7],[0],[7],[11],[2],[5],[1],[8],[6],[10],[5],[8],[7],[9],[0],[8],[7],[10],[9],[2],[7],[4],[7],[9],[4],[2],[5],[9],[8],[1],[11],[6],[6],[5],[6],[9],[9],[5],[8],[2],[9],[4],[7],[9],[9],[11],[9],[2],[3],[3],[7],[8],[0],[10],[0],[3],[10],[9],[10],[4],[11],[8],[1],[7],[11],[8],[4],[9],[10],[2],[0],[3],[4],[7],[11],[5],[7],[5],[9],[9],[11],[7],[5],[9],[3],[8],[4],[3],[10],[2],[1],[9],[7],[10],[5],[5],[3],[11],[9],[6],[7],[0],[11],[8],[1],[1],[2],[0],[4],[0],[8],[2],[3],[7],[4],[6],[10],[5],[5],[5],[2],[9],[3],[1],[8],[1],[4],[6],[11],[6],[2],[4],[9],[7],[3],[11],[5],[8],[7],[1],[8],[6],[8],[9],[8],[3],[5],[11],[2],[7],[4],[4],[8],[11],[1],[8],[3],[7],[3],[1],[0],[5],[9],[10],[10],[11],[6],[8],[1],[3],[10],[9],[0],[9],[9],[5],[8],[1],[4],[3],[7],[1],[5],[2],[5],[9],[9],[10],[2],[11],[1],[4],[11],[4],[9],[5],[9],[1],[0],[9],[2],[5],[8],[5],[1],[9],[10],[9],[2],[0],[0],[6],[11],[7],[10],[6],[10],[6],[8],[1],[10],[0],[5],[5],[7],[0],[11],[4],[10]],[[2],[7],[10],[9],[5],[9],[0],[6],[0],[11],[7],[8],[5],[9],[0],[1],[7],[7],[8],[4],[3],[11],[5],[2],[6],[9],[5],[3],[3],[4],[4],[7],[11],[3],[2],[2],[5],[6],[8],[5],[9],[2],[1],[7],[6],[4],[5],[10],[8],[10],[0],[0],[3],[0],[9],[5],[10],[5],[4],[2],[8],[11],[6],[8],[8],[6],[2],[7],[6],[11],[8],[1],[7],[5],[5],[4],[2],[3],[5],[10],[4],[11],[10],[11],[0],[8],[3],[8],[3],[4],[0],[9],[3],[2],[3],[1],[10],[9],[0],[11],[5],[11],[1],[5],[1],[6],[2],[1],[1],[3],[8],[2],[6],[0],[0],[5],[0],[5],[1],[1],[9],[7],[2],[10],[2],[5],[6],[9],[3],[5],[3],[10],[10],[1],[10],[10],[11],[0],[7],[3],[6],[10],[11],[11],[0],[1],[8],[5],[11],[10],[8],[1],[3],[6],[2],[4],[3],[11],[7],[5],[11],[10],[10],[9],[1],[10],[1],[8],[6],[0],[4],[5],[3],[4],[9],[0],[11],[8],[1],[1],[7],[8],[9],[0],[1],[5],[3],[10],[7],[10],[8],[5],[1],[4],[0],[1],[5],[10],[6],[2],[10],[6],[7],[8],[2],[3],[6],[9],[1],[10],[7],[9],[7],[6],[4],[0],[9],[10],[2],[10],[6],[7],[2],[0],[5],[3],[2],[9],[1],[11],[1],[5],[2],[6],[1],[2],[11],[10],[2],[10],[7],[5],[7],[5],[6],[7],[8],[8],[5],[8],[9],[3],[1],[11],[0],[0],[3],[8],[7],[10],[2],[10],[8],[8],[2],[6],[6],[10],[9],[5],[1],[4],[2],[4],[6],[10],[0],[2],[5],[10],[0],[4],[3],[11],[5],[8],[0],[11],[1],[0],[11],[5],[2],[4],[10],[2],[0],[1],[1],[3],[8],[6],[3],[8],[9],[6],[5],[1],[11],[2],[8],[9],[1],[10],[1],[1],[6],[4],[2],[6],[3],[0],[8],[2],[1],[9],[9],[3],[3],[4],[9],[10],[0],[1],[10],[2],[0],[10],[5],[2],[5],[1],[10],[4],[6],[2],[2],[10],[0],[0],[11],[11],[8],[10],[2],[6],[2],[8],[4],[7],[3],[2],[2],[9],[11],[9],[7],[6],[10],[8],[0],[10],[5],[7],[0],[7],[6],[2],[3],[4],[1],[7],[5],[4],[5],[9],[6],[1],[5],[7],[5],[8],[8],[6],[0],[0],[0],[2],[8],[4],[0],[4],[8],[9],[4],[1],[9],[1],[9],[11],[5],[3],[1],[0],[6],[4],[1],[2],[1],[5],[11],[11],[7],[4],[10],[8],[6],[6],[0],[5],[9],[0],[1],[5],[5],[4],[7],[4],[11],[9],[2],[4],[7],[0],[9],[7],[9],[3],[7],[9],[9],[2],[5],[7],[9],[0],[11],[11],[4],[10],[1],[1],[4],[9],[10],[10],[1],[6],[2],[10],[1],[7],[0],[4],[8],[0],[9],[0],[6],[6],[10],[0],[1],[0],[2],[5],[5],[3],[7],[7],[9],[8],[6],[10],[6],[5],[1],[9],[1],[7],[5],[9],[9],[2],[1],[3],[10],[9],[4],[6],[2],[1]],[[4],[3],[9],[10],[5],[6],[7],[9],[7],[7],[2],[8],[4],[5],[2],[5],[0],[7],[1],[0],[0],[1],[4],[11],[4],[9],[6],[6],[4],[5],[3],[4],[11],[4],[7],[5],[2],[4],[1],[10],[10],[11],[3],[9],[2],[3],[6],[5],[8],[11],[5],[10],[7],[3],[9],[2],[2],[5],[4],[4],[8],[0],[6],[2],[8],[10],[3],[8],[2],[4],[2],[5],[4],[3],[6],[2],[7],[7],[5],[11],[9],[10],[9],[11],[11],[5],[1],[9],[10],[2],[3],[7],[1],[9],[11],[0],[5],[9],[9],[2],[6],[8],[11],[3],[6],[3],[2],[10],[1],[9],[10],[1],[4],[8],[2],[4],[1],[2],[9],[3],[11],[2],[10],[9],[6],[8],[7],[8],[7],[11],[8],[6],[8],[5],[11],[9],[1],[8],[8],[9],[8],[6],[4],[9],[3],[7],[7],[9],[0],[8],[3],[3],[7],[1],[5],[3],[5],[4],[0],[8],[1],[5],[4],[5],[7],[6],[6],[8],[2],[3],[11],[3],[0],[0],[2],[8],[10],[2],[1],[4],[7],[4],[2],[4],[7],[2],[6],[11],[10],[10],[6],[7],[5],[11],[0],[0],[4],[6],[9],[0],[1],[5],[3],[9],[4],[4],[5],[7],[11],[0],[6],[7],[9],[10],[9],[10],[2],[3],[1],[9],[7],[0],[1],[1],[8],[3],[5],[9],[9],[3],[10],[8],[3],[3],[11],[5],[1],[4],[5],[10],[9],[0],[9],[6],[6],[11],[0],[6],[11],[6],[9],[10],[10],[5],[5],[1],[5],[10],[7],[9],[0],[6],[7],[11],[9],[5],[0],[8],[5],[7],[8],[2],[1],[3],[9],[9],[9],[3],[3],[0],[4],[10],[4],[6],[5],[2],[11],[11],[10],[3],[1],[8],[10],[9],[3],[8],[5],[3],[9],[10],[11],[3],[8],[7],[0],[3],[8],[0],[8],[0],[10],[11],[6],[0],[11],[2],[6],[11],[10],[6],[0],[0],[6],[10],[5],[5],[0],[10],[3],[10],[4],[4],[6],[4],[8],[11],[6],[9],[7],[8],[0],[8],[7],[10],[1],[2],[6],[4],[0],[6],[9],[2],[2],[8],[7],[3],[9],[9],[7],[11],[10],[4],[6],[6],[0],[2],[10],[2],[9],[6],[4],[6],[11],[10],[11],[9],[5],[8],[0],[7],[0],[6],[11],[3],[8],[3],[10],[0],[3],[8],[9],[7],[7],[7],[6],[7],[10],[10],[3],[0],[2],[0],[7],[4],[2],[0],[7],[3],[8],[0],[6],[6],[5],[0],[9],[11],[7],[9],[10],[3],[7],[11],[6],[9],[5],[9],[7],[8],[3],[11],[3],[8],[1],[11],[9],[6],[9],[7],[5],[8],[7],[3],[6],[11],[3],[4],[5],[10],[10],[3],[9],[11],[0],[6],[3],[1],[0],[6],[4],[7],[3],[9],[3],[7],[10],[5],[11],[11],[5],[5],[10],[4],[10],[7],[5],[1],[4],[3],[4],[8],[10],[7],[9],[2],[3],[9],[11],[5],[5],[4],[2],[4],[0],[9],[9],[0],[7],[3],[2],[11],[8],[5],[4],[7],[11],[10],[9],[6],[4],[8],[7],[7]],[[7],[7],[1],[10],[10],[5],[4],[2],[2],[2],[1],[10],[0],[0],[8],[2],[0],[5],[11],[0],[8],[4],[3],[8],[2],[11],[3],[11],[9],[1],[4],[1],[8],[0],[9],[11],[11],[9],[8],[1],[2],[2],[7],[2],[5],[0],[6],[6],[10],[2],[1],[1],[6],[8],[10],[3],[3],[3],[2],[8],[5],[11],[11],[4],[11],[8],[8],[3],[1],[7],[3],[11],[2],[1],[6],[4],[11],[7],[0],[10],[0],[5],[6],[8],[8],[2],[6],[8],[11],[6],[4],[9],[5],[9],[2],[10],[11],[9],[0],[4],[9],[5],[11],[4],[4],[10],[8],[8],[3],[4],[11],[1],[6],[11],[2],[9],[8],[10],[4],[1],[7],[6],[3],[1],[6],[8],[8],[0],[8],[0],[10],[9],[4],[6],[0],[1],[11],[8],[6],[11],[8],[0],[0],[8],[5],[2],[4],[11],[1],[6],[6],[11],[8],[4],[2],[7],[9],[8],[0],[9],[8],[5],[11],[8],[5],[2],[1],[3],[7],[0],[1],[1],[6],[4],[7],[4],[4],[10],[5],[9],[8],[0],[11],[0],[4],[11],[3],[1],[11],[4],[11],[6],[8],[10],[5],[7],[9],[11],[7],[5],[7],[5],[10],[11],[4],[7],[10],[10],[1],[10],[6],[7],[11],[7],[4],[5],[9],[8],[7],[6],[7],[7],[6],[0],[0],[0],[10],[9],[4],[2],[1],[10],[2],[1],[9],[1],[2],[2],[10],[8],[8],[10],[9],[7],[2],[9],[2],[11],[5],[11],[2],[1],[8],[8],[10],[2],[8],[1],[7],[7],[8],[9],[2],[9],[7],[7],[3],[9],[5],[9],[10],[11],[0],[9],[0],[11],[6],[3],[8],[2],[5],[5],[4],[8],[0],[3],[6],[7],[0],[9],[1],[4],[3],[2],[6],[0],[10],[7],[4],[7],[3],[0],[1],[11],[8],[8],[3],[3],[10],[2],[3],[11],[4],[0],[2],[8],[0],[9],[11],[4],[0],[8],[0],[6],[3],[6],[2],[7],[2],[2],[10],[11],[7],[1],[10],[2],[4],[0],[9],[9],[0],[5],[3],[6],[3],[9],[11],[4],[10],[11],[8],[10],[3],[2],[11],[8],[0],[3],[0],[9],[5],[9],[2],[0],[8],[8],[6],[4],[10],[9],[7],[10],[0],[0],[6],[6],[11],[10],[3],[3],[6],[4],[10],[1],[0],[11],[4],[10],[5],[6],[2],[5],[2],[10],[1],[11],[2],[6],[3],[0],[8],[7],[2],[3],[1],[4],[7],[3],[1],[10],[6],[3],[7],[5],[10],[8],[8],[4],[1],[4],[9],[9],[7],[1],[4],[11],[8],[5],[1],[6],[9],[7],[10],[4],[1],[5],[9],[1],[3],[1],[3],[5],[11],[6],[4],[11],[9],[8],[10],[1],[5],[4],[5],[9],[4],[8],[1],[1],[11],[9],[9],[0],[10],[5],[1],[8],[2],[7],[6],[3],[10],[11],[3],[0],[1],[11],[5],[9],[8],[3],[3],[4],[2],[0],[11],[7],[0],[9],[9],[9],[7],[8],[11],[0],[7],[5],[1],[11],[0],[4],[4],[3],[11],[1],[2],[7],[8],[0],[5],[11],[10],[7]],[[1],[0],[8],[5],[11],[3],[8],[6],[6],[11],[5],[11],[8],[4],[8],[2],[1],[4],[3],[5],[11],[1],[8],[5],[8],[10],[3],[1],[3],[1],[11],[5],[6],[11],[11],[0],[2],[0],[11],[9],[8],[3],[9],[0],[9],[9],[2],[11],[7],[10],[7],[4],[0],[5],[6],[8],[2],[7],[10],[4],[3],[1],[2],[3],[8],[9],[2],[7],[3],[5],[4],[1],[11],[9],[8],[10],[3],[9],[3],[10],[5],[3],[5],[11],[0],[8],[6],[11],[1],[0],[5],[9],[6],[10],[7],[10],[2],[11],[4],[10],[8],[6],[3],[4],[6],[11],[5],[11],[5],[10],[0],[10],[4],[8],[2],[11],[4],[9],[0],[8],[1],[2],[5],[2],[10],[11],[9],[2],[8],[9],[8],[0],[10],[11],[11],[3],[0],[4],[2],[0],[3],[2],[9],[6],[4],[10],[1],[8],[5],[9],[9],[7],[1],[3],[6],[9],[4],[10],[4],[0],[11],[2],[0],[9],[8],[8],[2],[9],[6],[0],[7],[2],[8],[11],[3],[11],[6],[2],[1],[2],[7],[6],[4],[2],[8],[1],[2],[6],[7],[11],[3],[0],[2],[6],[10],[6],[0],[3],[6],[7],[10],[9],[2],[8],[11],[7],[5],[11],[10],[9],[8],[5],[1],[6],[7],[2],[5],[6],[6],[11],[10],[8],[2],[10],[11],[2],[2],[0],[2],[9],[8],[5],[4],[1],[6],[0],[4],[4],[3],[2],[9],[3],[1],[4],[8],[10],[7],[7],[0],[3],[1],[8],[7],[6],[10],[0],[7],[4],[10],[8],[10],[5],[1],[4],[6],[10],[11],[9],[0],[11],[7],[9],[2],[1],[10],[8],[11],[0],[10],[3],[10],[11],[6],[9],[4],[9],[11],[2],[1],[2],[1],[8],[5],[4],[7],[4],[3],[6],[6],[4],[9],[10],[6],[5],[5],[6],[2],[5],[6],[3],[7],[5],[0],[4],[11],[8],[5],[6],[0],[4],[11],[3],[6],[7],[3],[2],[3],[0],[0],[7],[3],[9],[4],[10],[7],[6],[2],[5],[3],[10],[8],[0],[10],[11],[4],[9],[10],[11],[11],[9],[2],[9],[7],[9],[1],[9],[10],[5],[6],[6],[7],[0],[10],[10],[5],[4],[9],[0],[8],[8],[4],[6],[2],[4],[1],[3],[7],[0],[3],[0],[3],[7],[8],[1],[7],[6],[2],[10],[4],[6],[2],[1],[8],[1],[9],[0],[5],[4],[4],[10],[10],[9],[6],[11],[0],[6],[11],[10],[10],[3],[4],[11],[8],[4],[0],[3],[2],[4],[10],[2],[7],[10],[8],[11],[7],[4],[9],[8],[11],[7],[4],[11],[7],[3],[0],[5],[11],[5],[3],[6],[7],[2],[10],[3],[6],[4],[3],[6],[3],[3],[0],[9],[1],[9],[0],[10],[10],[8],[11],[9],[5],[8],[9],[8],[2],[2],[2],[9],[6],[3],[0],[2],[5],[5],[8],[11],[6],[7],[7],[8],[1],[3],[3],[2],[11],[9],[6],[8],[11],[10],[10],[6],[2],[1],[3],[6],[2],[5],[3],[1],[10],[0],[10],[0],[9],[10],[9],[7],[1],[7],[6],[3]]]
ZW = 548
def setup_inputs(rng):
    return {"z": rng.standard_normal((N, 128, ZW), dtype=np.float32)}
def reference(z):
    y = np.zeros((N, 128, T), np.float64)
    fill = [0] * N
    for r in range(N):
        for t in range(T):
            for e in ROUTE[r][t]:
                y[r][:, t] += z[e][:, fill[e]].astype(np.float64)
                fill[e] += 1
    return {"y": y.astype(z.dtype)}

@@ -1,0 +1,109 @@
+SCRATCH = {
+    "zs": ("sbuf", [128, 548], "float32"),
+    "rel": ("sbuf", [128, 548], "float32"),
+    "land": ("sbuf", [128, 512], "float32"),
+    "ybuf": ("sbuf", [128, 512], "float32"),
+}
+SEMAPHORES = ["ld", "sent", "relin", "scg", "scq", "st"] + ["a%d" % e for e in range(12)]
+
+GATE = {72: 74, 73: 75, 76: 78, 77: 79, 64: 70, 65: 71}
+
+
+def bits(m):
+    return bin(m).count("1")
+
+
+def rank_program(g, core, T, topo):
+    cores = list(T.cores)
+    n = len(cores)
+    route = T.tables["ROUTE"]
+    nt = T.tables["T"]
+
+    toks = [[[t for t in range(nt) if route[r][t][0] == e] for r in range(n)] for e in range(n)]
+    cnt = [[len(toks[e][r]) for r in range(n)] for e in range(n)]
+    off = [[sum(cnt[e][:r]) for r in range(n + 1)] for e in range(n)]
+    loff = [[sum(cnt[x][r] for x in range(e)) for e in range(n)] for r in range(n)]
+
+    rank = T.rank_of(core)
+    sent = [0]
+
+    def send(dst, out_ap, in_ap, sem):
+        rid, pid, _se = topo.addr(dst)
+        m = topo.mask(core, dst)
+        g.remote_dma(out_ap=out_ap, in_ap=in_ap, remote_sem=sem, local_sem=T.sem.sent,
+                     pid=pid, routing_id=rid, dma_engine_mask=m)
+        sent[0] += bits(m)
+
+    def far_ranks(e):
+        return [r for r in range(n) if topo.chip(cores[r]) != topo.chip(cores[e])]
+
+    if rank is not None:
+        e = rank
+        g.sync.dma_start(T.zs[:], T.z[:]).then_inc(T.sem.ld, 16)
+        g.wait_ge(T.sem.ld, 16)
+        far = far_ranks(e)
+        if core in GATE:
+            a, b = off[e][far[0]], off[e][far[-1] + 1]
+            send(GATE[core], T.rel[:, 0:b - a], T.zs[:, a:b], T.sem.relin)
+        else:
+            for r in far:
+                if cnt[e][r]:
+                    send(cores[r], T.land[:, loff[r][e]:loff[r][e] + cnt[e][r]],
+                         T.zs[:, off[e][r]:off[e][r + 1]], T.sem["a%d" % e])
+        for k in range(1, n):
+            r = (e + k) % n
+            if r not in far and cnt[e][r]:
+                send(cores[r], T.land[:, loff[r][e]:loff[r][e] + cnt[e][r]],
+                     T.zs[:, off[e][r]:off[e][r + 1]], T.sem["a%d" % e])
+
+    for src, gate in GATE.items():
+        if gate != core:
+            continue
+        e = T.rank_of(src)
+        far = far_ranks(e)
+        base = off[e][far[0]]
+        g.wait_ge(T.sem.relin, bits(topo.mask(src, core)))
+        for r in far:
+            if cnt[e][r]:
+                send(cores[r], T.land[:, loff[r][e]:loff[r][e] + cnt[e][r]],
+                     T.rel[:, off[e][r] - base:off[e][r + 1] - base], T.sem["a%d" % e])
+
+    if rank is None:
+        if sent[0]:
+            g.wait_ge(T.sem.sent, sent[0])
+        return
+
+    r = rank
+    queues = [g.sync, g.scalar, g]
+    issued = [0, 0, 0]
+    turn = 0
+    near = [x for x in range(n) if x != r and topo.chip(cores[x]) == topo.chip(core)]
+    farx = [x for x in range(n) if topo.chip(cores[x]) != topo.chip(core)]
+    for e in [r] + near + farx:
+        if not cnt[e][r]:
+            continue
+        if e == r:
+            buf, base, sem, need = T.zs, off[r][r], T.sem.ld, 16
+        else:
+            last = GATE.get(cores[e], cores[e]) if e in farx else cores[e]
+            buf, base, sem, need = T.land, loff[r][e], T.sem["a%d" % e], bits(topo.mask(last, core))
+        for q in queues:
+            q.wait_ge(sem, need)
+        ts = toks[e][r]
+        i = 0
+        while i < len(ts):
+            j = i + 1
+            while j < len(ts) and ts[j] == ts[j - 1] + 1:
+                j += 1
+            q = queues[turn]
+            q.dma_start(T.ybuf[:, ts[i]:ts[i] + j - i], buf[:, base + i:base + j]).then_inc(
+                T.sem.scg if turn == 2 else T.sem.scq, 16)
+            issued[turn] += 1
+            turn = (turn + 1) % 3
+            i = j
+
+    g.wait_ge(T.sem.scg, 16 * issued[2])
+    g.wait_ge(T.sem.scq, 16 * (issued[0] + issued[1]))
+    g.dma_start(T.y[:], T.ybuf[:]).then_inc(T.sem.st, 16)
+    g.wait_ge(T.sem.st, 16)
+    g.wait_ge(T.sem.sent, sent[0])

@@ -4,13 +4,53 @@ SCRATCH = {
     "land": ("sbuf", [128, 512], "float32"),
     "ybuf": ("sbuf", [128, 512], "float32"),
 }
-SEMAPHORES = ["ld", "sent", "relin", "scg", "scq", "st"] + ["a%d" % e for e in range(12)]
-
-GATE = {72: 74, 73: 75, 76: 78, 77: 79, 64: 70, 65: 71}
+SEMAPHORES = ["ld", "sent", "h0", "h1", "h2", "scg", "scq", "st"] + ["a%d" % e for e in range(12)]
 
 
 def bits(m):
     return bin(m).count("1")
+
+
+def plan(cores, cnt, off, nt, topo):
+    n = len(cores)
+    hand, all_owners = [], []
+    for c in sorted(set(topo.chip(x) for x in cores)):
+        here = [e for e in range(n) if topo.chip(cores[e]) == c]
+        far = [r for r in range(n) if topo.chip(cores[r]) != c]
+        owners = [x for x in range(8 * c, 8 * c + 8) if topo.may_write(x, cores[far[0]])]
+        all_owners += owners
+        span = dict((e, (off[e][far[0]], off[e][far[-1] + 1])) for e in here)
+        givers = [e for e in here if cores[e] not in owners]
+        busy = dict((o, 0) for o in owners)
+        port = {0: 0, 1: 0}
+        for o in owners:
+            if o in cores:
+                e = cores.index(o)
+                busy[o] = max(off[e][n], nt) - cnt[e][e]
+                port[topo.die(o)] += span[e][1] - span[e][0]
+        total = sum(span[e][1] - span[e][0] for e in givers)
+        d0 = topo.die(cores[givers[0]])
+        quota = {}
+        quota[d0] = min(max((port[0] + port[1] + total + 1) // 2 - port[d0], 0), total)
+        quota[1 - d0] = total - quota[d0]
+        share = []
+        for d in (d0, 1 - d0):
+            o1, o2 = [o for o in owners if topo.die(o) == d]
+            f1 = min(max((quota[d] + busy[o2] - busy[o1] + 1) // 2, 0), quota[d])
+            share += [(o1, f1), (o2, quota[d] - f1)]
+        givers.sort(key=lambda e: (topo.die(cores[e]) != d0, e))
+        gi, pos = 0, span[givers[0]][0]
+        for o, f in share:
+            while f:
+                e = givers[gi]
+                k = min(f, span[e][1] - pos)
+                hand.append((e, o, pos, pos + k))
+                pos += k
+                f -= k
+                if pos == span[e][1] and gi + 1 < len(givers):
+                    gi += 1
+                    pos = span[givers[gi]][0]
+    return hand, all_owners
 
 
 def rank_program(g, core, T, topo):
@@ -23,50 +63,64 @@ def rank_program(g, core, T, topo):
     cnt = [[len(toks[e][r]) for r in range(n)] for e in range(n)]
     off = [[sum(cnt[e][:r]) for r in range(n + 1)] for e in range(n)]
     loff = [[sum(cnt[x][r] for x in range(e)) for e in range(n)] for r in range(n)]
+    hand, owners = plan(cores, cnt, off, nt, topo)
+
+    def mask(src, dst):
+        if topo.chip(src) != topo.chip(dst):
+            return 0x00FF
+        return 0xFF00 if src in owners else 0xFFFF
+
+    finals = []
+    for e in range(n):
+        for r in range(n):
+            if r == e or not cnt[e][r]:
+                continue
+            if topo.chip(cores[e]) == topo.chip(cores[r]) or cores[e] in owners:
+                finals.append((cores[e], e, r, off[e][r], off[e][r + 1], off[e][r]))
+    fill = dict((o, 0) for o in owners)
+    slot = []
+    nth = dict((o, 0) for o in owners)
+    for e, o, lo, hi in hand:
+        slot.append((fill[o], nth[o]))
+        for r in range(n):
+            a, b = max(lo, off[e][r]), min(hi, off[e][r + 1])
+            if a < b:
+                finals.append((o, e, r, a, b, fill[o] + a - lo))
+        fill[o] += hi - lo
+        nth[o] += 1
 
     rank = T.rank_of(core)
     sent = [0]
 
     def send(dst, out_ap, in_ap, sem):
         rid, pid, _se = topo.addr(dst)
-        m = topo.mask(core, dst)
+        m = mask(core, dst)
         g.remote_dma(out_ap=out_ap, in_ap=in_ap, remote_sem=sem, local_sem=T.sem.sent,
                      pid=pid, routing_id=rid, dma_engine_mask=m)
         sent[0] += bits(m)
 
-    def far_ranks(e):
-        return [r for r in range(n) if topo.chip(cores[r]) != topo.chip(cores[e])]
+    def deliver(buf, w):
+        _s, e, r, lo, hi, col = w
+        at = loff[r][e] + lo - off[e][r]
+        send(cores[r], T.land[:, at:at + hi - lo], buf[:, col:col + hi - lo], T.sem["a%d" % e])
 
     if rank is not None:
-        e = rank
         g.sync.dma_start(T.zs[:], T.z[:]).then_inc(T.sem.ld, 16)
         g.wait_ge(T.sem.ld, 16)
-        far = far_ranks(e)
-        if core in GATE:
-            a, b = off[e][far[0]], off[e][far[-1] + 1]
-            send(GATE[core], T.rel[:, 0:b - a], T.zs[:, a:b], T.sem.relin)
-        else:
-            for r in far:
-                if cnt[e][r]:
-                    send(cores[r], T.land[:, loff[r][e]:loff[r][e] + cnt[e][r]],
-                         T.zs[:, off[e][r]:off[e][r + 1]], T.sem["a%d" % e])
-        for k in range(1, n):
-            r = (e + k) % n
-            if r not in far and cnt[e][r]:
-                send(cores[r], T.land[:, loff[r][e]:loff[r][e] + cnt[e][r]],
-                     T.zs[:, off[e][r]:off[e][r + 1]], T.sem["a%d" % e])
+        for i, (e, o, lo, hi) in enumerate(hand):
+            if e == rank:
+                send(o, T.rel[:, slot[i][0]:slot[i][0] + hi - lo], T.zs[:, lo:hi], T.sem["h%d" % slot[i][1]])
+        mine = [w for w in finals if w[0] == core and w[1] == rank]
+        mine.sort(key=lambda w: (topo.chip(cores[w[2]]) == topo.chip(core), (w[2] - rank) % n))
+        for w in mine:
+            deliver(T.zs, w)
 
-    for src, gate in GATE.items():
-        if gate != core:
-            continue
-        e = T.rank_of(src)
-        far = far_ranks(e)
-        base = off[e][far[0]]
-        g.wait_ge(T.sem.relin, bits(topo.mask(src, core)))
-        for r in far:
-            if cnt[e][r]:
-                send(cores[r], T.land[:, loff[r][e]:loff[r][e] + cnt[e][r]],
-                     T.rel[:, off[e][r] - base:off[e][r + 1] - base], T.sem["a%d" % e])
+    for i, (e, o, lo, hi) in enumerate(hand):
+        if o == core:
+            g.wait_ge(T.sem["h%d" % slot[i][1]], bits(mask(cores[e], core)))
+            for w in finals:
+                if w[0] == core and w[1] == e and lo <= w[3] < hi:
+                    deliver(T.rel, w)
 
     if rank is None:
         if sent[0]:
@@ -77,16 +131,18 @@ def rank_program(g, core, T, topo):
     queues = [g.sync, g.scalar, g]
     issued = [0, 0, 0]
     turn = 0
-    near = [x for x in range(n) if x != r and topo.chip(cores[x]) == topo.chip(core)]
-    farx = [x for x in range(n) if topo.chip(cores[x]) != topo.chip(core)]
-    for e in [r] + near + farx:
+    near = [(r - k) % n for k in range(1, n)]
+    near = [x for x in near if topo.chip(cores[x]) == topo.chip(core)]
+    direct = [x for x in range(n) if topo.chip(cores[x]) != topo.chip(core) and cores[x] in owners]
+    relayed = [x for x in range(n) if topo.chip(cores[x]) != topo.chip(core) and cores[x] not in owners]
+    for e in [r] + near + direct + relayed:
         if not cnt[e][r]:
             continue
         if e == r:
             buf, base, sem, need = T.zs, off[r][r], T.sem.ld, 16
         else:
-            last = GATE.get(cores[e], cores[e]) if e in farx else cores[e]
-            buf, base, sem, need = T.land, loff[r][e], T.sem["a%d" % e], bits(topo.mask(last, core))
+            buf, base, sem = T.land, loff[r][e], T.sem["a%d" % e]
+            need = sum(bits(mask(w[0], core)) for w in finals if w[1] == e and w[2] == r)
         for q in queues:
             q.wait_ge(sem, need)
         ts = toks[e][r]
@@ -95,8 +151,7 @@ def rank_program(g, core, T, topo):
             j = i + 1
             while j < len(ts) and ts[j] == ts[j - 1] + 1:
                 j += 1
-            q = queues[turn]
-            q.dma_start(T.ybuf[:, ts[i]:ts[i] + j - i], buf[:, base + i:base + j]).then_inc(
+            queues[turn].dma_start(T.ybuf[:, ts[i]:ts[i] + j - i], buf[:, base + i:base + j]).then_inc(
                 T.sem.scg if turn == 2 else T.sem.scq, 16)
             issued[turn] += 1
             turn = (turn + 1) % 3

SCRATCH = {
    "zs": ("sbuf", [128, 548], "float32"),
    "rel": ("sbuf", [128, 548], "float32"),
    "land": ("sbuf", [128, 512], "float32"),
    "ybuf": ("sbuf", [128, 512], "float32"),
}
SEMAPHORES = ["ld", "sent", "h0", "h1", "h2", "scg", "scq", "st"] + ["a%d" % e for e in range(12)]


def bits(m):
    return bin(m).count("1")


def plan(cores, cnt, off, nt, topo):
    n = len(cores)
    hand, all_owners = [], []
    for c in sorted(set(topo.chip(x) for x in cores)):
        here = [e for e in range(n) if topo.chip(cores[e]) == c]
        far = [r for r in range(n) if topo.chip(cores[r]) != c]
        owners = [x for x in range(8 * c, 8 * c + 8) if topo.may_write(x, cores[far[0]])]
        all_owners += owners
        span = dict((e, (off[e][far[0]], off[e][far[-1] + 1])) for e in here)
        givers = [e for e in here if cores[e] not in owners]
        busy = dict((o, 0) for o in owners)
        port = {0: 0, 1: 0}
        for o in owners:
            if o in cores:
                e = cores.index(o)
                busy[o] = max(off[e][n], nt) - cnt[e][e]
                port[topo.die(o)] += span[e][1] - span[e][0]
        total = sum(span[e][1] - span[e][0] for e in givers)
        d0 = topo.die(cores[givers[0]])
        quota = {}
        quota[d0] = min(max((port[0] + port[1] + total + 1) // 2 - port[d0], 0), total)
        quota[1 - d0] = total - quota[d0]
        share = []
        for d in (d0, 1 - d0):
            o1, o2 = [o for o in owners if topo.die(o) == d]
            f1 = min(max((quota[d] + busy[o2] - busy[o1] + 1) // 2, 0), quota[d])
            share += [(o1, f1), (o2, quota[d] - f1)]
        givers.sort(key=lambda e: (topo.die(cores[e]) != d0, e))
        gi, pos = 0, span[givers[0]][0]
        for o, f in share:
            while f:
                e = givers[gi]
                k = min(f, span[e][1] - pos)
                hand.append((e, o, pos, pos + k))
                pos += k
                f -= k
                if pos == span[e][1] and gi + 1 < len(givers):
                    gi += 1
                    pos = span[givers[gi]][0]
    return hand, all_owners


def rank_program(g, core, T, topo):
    cores = list(T.cores)
    n = len(cores)
    route = T.tables["ROUTE"]
    nt = T.tables["T"]

    toks = [[[t for t in range(nt) if route[r][t][0] == e] for r in range(n)] for e in range(n)]
    cnt = [[len(toks[e][r]) for r in range(n)] for e in range(n)]
    off = [[sum(cnt[e][:r]) for r in range(n + 1)] for e in range(n)]
    loff = [[sum(cnt[x][r] for x in range(e)) for e in range(n)] for r in range(n)]
    hand, owners = plan(cores, cnt, off, nt, topo)

    def mask(src, dst):
        if topo.chip(src) != topo.chip(dst):
            return 0x00FF
        return 0xFF00 if src in owners else 0xFFFF

    finals = []
    for e in range(n):
        for r in range(n):
            if r == e or not cnt[e][r]:
                continue
            if topo.chip(cores[e]) == topo.chip(cores[r]) or cores[e] in owners:
                finals.append((cores[e], e, r, off[e][r], off[e][r + 1], off[e][r]))
    fill = dict((o, 0) for o in owners)
    slot = []
    nth = dict((o, 0) for o in owners)
    for e, o, lo, hi in hand:
        slot.append((fill[o], nth[o]))
        for r in range(n):
            a, b = max(lo, off[e][r]), min(hi, off[e][r + 1])
            if a < b:
                finals.append((o, e, r, a, b, fill[o] + a - lo))
        fill[o] += hi - lo
        nth[o] += 1

    rank = T.rank_of(core)
    sent = [0]

    def send(dst, out_ap, in_ap, sem):
        rid, pid, _se = topo.addr(dst)
        m = mask(core, dst)
        g.remote_dma(out_ap=out_ap, in_ap=in_ap, remote_sem=sem, local_sem=T.sem.sent,
                     pid=pid, routing_id=rid, dma_engine_mask=m)
        sent[0] += bits(m)

    def deliver(buf, w):
        _s, e, r, lo, hi, col = w
        at = loff[r][e] + lo - off[e][r]
        send(cores[r], T.land[:, at:at + hi - lo], buf[:, col:col + hi - lo], T.sem["a%d" % e])

    if rank is not None:
        g.sync.dma_start(T.zs[:], T.z[:]).then_inc(T.sem.ld, 16)
        g.wait_ge(T.sem.ld, 16)
        for i, (e, o, lo, hi) in enumerate(hand):
            if e == rank:
                send(o, T.rel[:, slot[i][0]:slot[i][0] + hi - lo], T.zs[:, lo:hi], T.sem["h%d" % slot[i][1]])
        mine = [w for w in finals if w[0] == core and w[1] == rank]
        mine.sort(key=lambda w: (topo.chip(cores[w[2]]) == topo.chip(core), (w[2] - rank) % n))
        for w in mine:
            deliver(T.zs, w)

    for i, (e, o, lo, hi) in enumerate(hand):
        if o == core:
            g.wait_ge(T.sem["h%d" % slot[i][1]], bits(mask(cores[e], core)))
            for w in finals:
                if w[0] == core and w[1] == e and lo <= w[3] < hi:
                    deliver(T.rel, w)

    if rank is None:
        if sent[0]:
            g.wait_ge(T.sem.sent, sent[0])
        return

    r = rank
    queues = [g.sync, g.scalar, g]
    issued = [0, 0, 0]
    turn = 0
    near = [(r - k) % n for k in range(1, n)]
    near = [x for x in near if topo.chip(cores[x]) == topo.chip(core)]
    direct = [x for x in range(n) if topo.chip(cores[x]) != topo.chip(core) and cores[x] in owners]
    relayed = [x for x in range(n) if topo.chip(cores[x]) != topo.chip(core) and cores[x] not in owners]
    for e in [r] + near + direct + relayed:
        if not cnt[e][r]:
            continue
        if e == r:
            buf, base, sem, need = T.zs, off[r][r], T.sem.ld, 16
        else:
            buf, base, sem = T.land, loff[r][e], T.sem["a%d" % e]
            need = sum(bits(mask(w[0], core)) for w in finals if w[1] == e and w[2] == r)
        for q in queues:
            q.wait_ge(sem, need)
        ts = toks[e][r]
        i = 0
        while i < len(ts):
            j = i + 1
            while j < len(ts) and ts[j] == ts[j - 1] + 1:
                j += 1
            queues[turn].dma_start(T.ybuf[:, ts[i]:ts[i] + j - i], buf[:, base + i:base + j]).then_inc(
                T.sem.scg if turn == 2 else T.sem.scq, 16)
            issued[turn] += 1
            turn = (turn + 1) % 3
            i = j

    g.wait_ge(T.sem.scg, 16 * issued[2])
    g.wait_ge(T.sem.scq, 16 * (issued[0] + issued[1]))
    g.dma_start(T.y[:], T.ybuf[:]).then_inc(T.sem.st, 16)
    g.wait_ge(T.sem.st, 16)
    g.wait_ge(T.sem.sent, sent[0])
